import numpy as np
import ml_dtypes


def mxq(x, axis, fmt="e4m3"):
    dtype, down = {"e4m3": (ml_dtypes.float8_e4m3fn, 7), "e5m2": (ml_dtypes.float8_e5m2, 14)}[fmt]
    v = np.moveaxis(np.asarray(x, np.float32).astype(ml_dtypes.bfloat16).astype(np.float64), axis, -1)
    blocks = v.reshape(v.shape[:-1] + (-1, 32))
    amax = np.abs(blocks).max(-1, keepdims=True)
    byte = np.maximum(np.where(amax > 0, np.frexp(amax)[1] - 1 + 127, 0) - down, 1)
    scale = np.exp2(byte - 127.0)
    codes = (blocks / scale).astype(np.float32).astype(dtype).astype(np.float64)
    return np.moveaxis((codes * scale).reshape(v.shape), -1, axis)


WIDE = False


def mx_kscale(k):
    if not WIDE:
        return np.ones(k)
    levels = np.array([10, -10, 5, -5, 0])
    if k % 512:
        return np.exp2(np.random.permutation(np.resize(levels, k // 32))).repeat(32)
    a = np.empty((k // 512, 16))
    for p in range(k // 512):
        a[p, :8] = np.random.permutation(np.resize(levels, 8))
        for g in range(8):
            far = levels[np.abs(levels - a[p, g]) >= 10]
            a[p, g + 8] = far[np.random.randint(len(far))]
    return np.exp2(a.ravel()).repeat(32)


def f64(x):
    return np.asarray(x).astype(np.float64)


def striped(idx):
    return np.tile(idx.reshape(-1, 16).T, (8, 1)).astype(np.uint16)


def unstriped(offs):
    return offs[:16].T.reshape(-1).astype(np.int64)


def relu2(v):
    return np.maximum(v, 0.0) ** 2


K, T, S, H, N = 1024, 2048, 768, 512, 512


def setup_inputs():
    n = np.random.standard_normal
    s = mx_kscale(K)[:, None]
    u = mx_kscale(H)
    return {
        "xT": (n((K, T)) * s).astype(np.float32),
        "w1": (n((K, H)) / np.sqrt(K) / s * u).astype(np.float32),
        "w2": (n((H, N)) / np.sqrt(H) / u[:, None] ** 2).astype(np.float32),
        "offs": striped(np.sort(np.random.permutation(T)[:S])),
    }


def reference(xT, w1, w2, offs):
    idx = unstriped(offs)
    xq = mxq(f64(xT)[:, idx], 0, "e4m3")
    h = relu2(mxq(f64(w1), 0, "e4m3").T @ xq)
    y = mxq(f64(w2), 0, "e4m3").T @ mxq(h, 0, "e4m3")
    return y

@@ -1,0 +1,240 @@
+from contextlib import ExitStack
+
+import concourse.mybir as mybir
+
+K, T, S, H, N = 1024, 2048, 768, 512, 512
+FLOPS = 2 * S * (K * H + H * N)
+
+F32 = mybir.dt.float32
+BF16 = mybir.dt.bfloat16
+U32 = mybir.dt.uint32
+U16 = mybir.dt.uint16
+U8 = mybir.dt.uint8
+FP8X4 = mybir.dt.float8_e4m3fn_x4
+SQUARE = mybir.ActivationFunctionType.Square
+RELU = mybir.ActivationFunctionType.Relu
+MULT = mybir.AluOpType.mult
+
+P = 128
+CH = 256
+NCH = S // CH
+HEAD = 1536
+
+
+def tile_picked_pick_mlp_relu2_srt_e_kernel(tc, xT, w1, w2, offs, out):
+    nc = tc.nc
+    with ExitStack() as ctx:
+        lists = ctx.enter_context(tc.tile_pool(name="lists", bufs=1))
+        keep = ctx.enter_context(tc.tile_pool(name="keep", bufs=1))
+        psum = ctx.enter_context(tc.psum_pool(name="psum", bufs=8))
+
+        offs_t = lists.tile([P, S // 16], U16, name="offs_t")
+        nc.sync.dma_start(offs_t[:], offs)
+
+        xv = xT.rearrange("(s p j) t -> s j p t", s=2, j=4)
+        w1v = w1.rearrange("(s p j) c -> s p j c", s=2, j=4)
+        w2v = w2.rearrange("(p j) c -> p j c", j=4)
+
+        x = [[keep.tile([P, T], F32, name="x%d%d" % (s, j)) for j in range(4)] for s in range(2)]
+        w1r = [keep.tile([P, 4, H], F32, name="w1r%d" % s) for s in range(2)]
+        w2r = [keep.tile([P, 4, N // 2], F32, name="w2r%d" % h) for h in range(2)]
+
+        nc.sync.dma_start(w1r[0][:], w1v[0])
+        nc.sync.dma_start(x[0][0][:], xv[0, 0])
+        nc.sync.dma_start(x[0][1][:], xv[0, 1])
+        nc.sync.dma_start(x[0][2][:], xv[0, 2])
+        nc.sync.dma_start(x[0][3][:], xv[0, 3])
+        nc.sync.dma_start(x[1][0][:], xv[1, 0])
+        nc.sync.dma_start(w1r[1][:], w1v[1])
+        nc.sync.dma_start(x[1][1][:], xv[1, 1])
+        nc.sync.dma_start(x[1][2][:], xv[1, 2])
+        nc.sync.dma_start(x[1][3][:, 0:HEAD], xv[1, 3][:, 0:HEAD])
+        nc.sync.dma_start(w2r[0][:], w2v[:, :, 0:256])
+        nc.sync.dma_start(x[1][3][:, HEAD:T], xv[1, 3][:, HEAD:T])
+        nc.sync.dma_start(w2r[1][:], w2v[:, :, 256:512])
+
+        g0 = keep.tile([P, 4, S], F32, name="g0")
+        xb = [keep.tile([P, S, 4], BF16, name="xb%d" % s, align_bytes=64) for s in range(2)]
+        xc = [keep.tile([P, S], U32, name="xc%d" % s, align_bytes=64) for s in range(2)]
+        xs = [keep.tile([P, S], U8, name="xs%d" % s, align_bytes=64) for s in range(2)]
+        w1b = [keep.tile([P, H * 4], BF16, name="w1b%d" % s, align_bytes=64) for s in range(2)]
+        w1c = [keep.tile([P, H], U32, name="w1c%d" % s, align_bytes=64) for s in range(2)]
+        w1s = [keep.tile([P, H], U8, name="w1s%d" % s, align_bytes=64) for s in range(2)]
+        w2b = [keep.tile([P, N // 2, 4], BF16, name="w2b%d" % h, align_bytes=64) for h in range(2)]
+        w2c = [keep.tile([P, N // 2], U32, name="w2c%d" % h, align_bytes=64) for h in range(2)]
+        w2s = [keep.tile([P, N // 2], U8, name="w2s%d" % h, align_bytes=64) for h in range(2)]
+        r = [keep.tile([P, 4, CH], F32, name="r%d" % c) for c in range(NCH)]
+        hb = [keep.tile([P, CH, 4], BF16, name="hb%d" % c, align_bytes=64) for c in range(NCH)]
+        hc = [keep.tile([P, CH], U32, name="hc%d" % c, align_bytes=64) for c in range(NCH)]
+        hs = [keep.tile([P, CH], U8, name="hs%d" % c, align_bytes=64) for c in range(NCH)]
+        y = [[keep.tile([P, 2, CH], F32, name="y%d%d" % (c, b)) for b in range(2)] for c in range(NCH)]
+
+        def cols(c):
+            return slice(CH * c, CH * (c + 1))
+
+        def interleave(copy, dst, src):
+            copy(
+                out=dst.rearrange("p (c i) t -> p c t i", i=4),
+                in_=src.rearrange("p t (c i) -> p c t i", i=4),
+            )
+
+        def w1_copy(s, h, copy):
+            ms = slice(64 * h, 64 * (h + 1))
+            copy(
+                out=w1b[s][:].rearrange("p (t m j) -> p m j t", t=4, j=4)[:, ms],
+                in_=w1r[s][:].rearrange("p j (m t) -> p m j t", t=4)[:, ms],
+            )
+
+        def w1_quant(s):
+            nc.vector.quantize_mx(out=w1c[s][:].bitcast(FP8X4), scales=w1s[s][:], in_=w1b[s][:])
+
+        def x_quant(s, c):
+            nc.vector.quantize_mx(
+                out=xc[s][:, cols(c)].bitcast(FP8X4),
+                scales=xs[s][:, cols(c)],
+                in_=xb[s][:, cols(c), :].rearrange("p n t -> p (n t)"),
+            )
+
+        def gather0(j):
+            nc.vector.tensor_copy(g0[:, j, :], x[0][j][:].indirect(offs_t[:]))
+
+        def gather1(j):
+            nc.vector.tensor_copy(xb[1][:, :, j], x[1][j][:].indirect(offs_t[:]))
+
+        def gather_part(j, c):
+            width = HEAD if c == 0 else T
+            nc.vector.tensor_copy(
+                xb[1][:, cols(c), j],
+                x[1][j][:, 0:width].indirect(offs_t[:, CH // 16 * c : CH // 16 * (c + 1)]),
+            )
+
+        def w2_quant(h):
+            nc.vector.quantize_mx(
+                out=w2c[h][:].bitcast(FP8X4),
+                scales=w2s[h][:],
+                in_=w2b[h][:].rearrange("p n t -> p (n t)"),
+            )
+
+        def mm1(c, b):
+            bank = psum.tile([P, 2, CH], F32, name="bank")
+            for i in range(2):
+                t = 2 * b + i
+                for s in range(2):
+                    nc.tensor.matmul_mx(
+                        out=bank[:, i, :],
+                        lhsT=w1c[s][:, P * t : P * (t + 1)].bitcast(FP8X4),
+                        lhsT_scale=w1s[s][:, P * t : P * (t + 1)],
+                        rhs=xc[s][:, cols(c)].bitcast(FP8X4),
+                        rhs_scale=xs[s][:, cols(c)],
+                        start=(s == 0),
+                        stop=(s == 1),
+                    )
+            return bank
+
+        def relu(c, b, bank, on_vector):
+            if on_vector:
+                nc.vector.tensor_scalar_max(r[c][:, 2 * b : 2 * b + 2, :], bank[:], 0.0)
+            else:
+                nc.scalar.activation(r[c][:, 2 * b : 2 * b + 2, :], bank[:], RELU)
+
+        def square(c, h, on_vector):
+            n = slice(CH // 2 * h, CH // 2 * (h + 1))
+            rv = r[c][:, :, n].rearrange("p t (c i) -> p c t i", i=4)
+            hv = hb[c][:, n, :].rearrange("p (c i) t -> p c t i", i=4)
+            if on_vector:
+                nc.vector.tensor_tensor(hv, rv, rv, MULT)
+            else:
+                nc.scalar.activation(hv, rv, SQUARE)
+
+        def h_quant(c):
+            nc.vector.quantize_mx(
+                out=hc[c][:].bitcast(FP8X4),
+                scales=hs[c][:],
+                in_=hb[c][:].rearrange("p n t -> p (n t)"),
+            )
+
+        def mm2(c, b):
+            bank = psum.tile([P, 2, CH], F32, name="bank")
+            for i in range(2):
+                nc.tensor.matmul_mx(
+                    out=bank[:, i, :],
+                    lhsT=w2c[b][:, P * i : P * (i + 1)].bitcast(FP8X4),
+                    lhsT_scale=w2s[b][:, P * i : P * (i + 1)],
+                    rhs=hc[c][:].bitcast(FP8X4),
+                    rhs_scale=hs[c][:],
+                    start=True,
+                    stop=True,
+                )
+            return bank
+
+        ov = out.rearrange("(b i p) n -> b p i n", b=2, i=2)
+        b1, b2 = {}, {}
+
+        w1_copy(0, 0, nc.vector.tensor_copy)
+        w1_copy(0, 1, nc.scalar.copy)
+        gather0(0)
+        w1_quant(0)
+        gather0(1)
+        gather0(2)
+        gather0(3)
+        interleave(nc.scalar.copy, xb[0][:, cols(0), :], g0[:, :, cols(0)])
+        interleave(nc.vector.tensor_copy, xb[0][:, cols(1), :], g0[:, :, cols(1)])
+        interleave(nc.scalar.copy, xb[0][:, cols(2), :], g0[:, :, cols(2)])
+        gather1(0)
+        w1_copy(1, 0, nc.vector.tensor_copy)
+        w1_copy(1, 1, nc.scalar.copy)
+        x_quant(0, 0)
+        x_quant(0, 1)
+        x_quant(0, 2)
+        w1_quant(1)
+        gather1(1)
+        gather1(2)
+        gather_part(3, 0)
+        x_quant(1, 0)
+        interleave(nc.scalar.copy, w2b[0][:], w2r[0][:])
+        b1[0,0] = mm1(0, 0)
+        b1[0,1] = mm1(0, 1)
+        gather_part(3, 1)
+        relu(0, 0, b1[0,0], False)
+        gather_part(3, 2)
+        relu(0, 1, b1[0,1], False)
+        x_quant(1, 1)
+        b1[1,0] = mm1(1, 0)
+        b1[1,1] = mm1(1, 1)
+        interleave(nc.vector.tensor_copy, w2b[1][:], w2r[1][:])
+        x_quant(1, 2)
+        square(0, 0, False)
+        square(0, 1, False)
+        relu(1, 0, b1[1,0], False)
+        relu(1, 1, b1[1,1], True)
+        b1[2,0] = mm1(2, 0)
+        b1[2,1] = mm1(2, 1)
+        w2_quant(0)
+        w2_quant(1)
+        h_quant(0)
+        square(1, 0, True)
+        square(1, 1, False)
+        relu(2, 0, b1[2,0], False)
+        relu(2, 1, b1[2,1], True)
+        b2[0,0] = mm2(0, 0)
+        b2[0,1] = mm2(0, 1)
+        h_quant(1)
+        nc.scalar.copy(y[0][0][:], b2[0,0][:])
+        nc.vector.tensor_copy(y[0][1][:], b2[0,1][:])
+        nc.sync.dma_start(ov[0][:, :, cols(0)], y[0][0][:])
+        nc.sync.dma_start(ov[1][:, :, cols(0)], y[0][1][:])
+        square(2, 0, False)
+        square(2, 1, True)
+        b2[1,0] = mm2(1, 0)
+        b2[1,1] = mm2(1, 1)
+        nc.scalar.copy(y[1][0][:], b2[1,0][:])
+        nc.vector.tensor_copy(y[1][1][:], b2[1,1][:])
+        nc.sync.dma_start(ov[0][:, :, cols(1)], y[1][0][:])
+        nc.sync.dma_start(ov[1][:, :, cols(1)], y[1][1][:])
+        h_quant(2)
+        b2[2,0] = mm2(2, 0)
+        b2[2,1] = mm2(2, 1)
+        nc.vector.tensor_copy(y[2][0][:], b2[2,0][:])
+        nc.scalar.copy(y[2][1][:], b2[2,1][:])
+        nc.sync.dma_start(ov[0][:, :, cols(2)], y[2][0][:])
+        nc.sync.dma_start(ov[1][:, :, cols(2)], y[2][1][:])

@@ -37,11 +37,11 @@ def tile_picked_pick_mlp_relu2_srt_e_kernel(tc, xT, w1, w2, offs, out):
 
         x = [[keep.tile([P, T], F32, name="x%d%d" % (s, j)) for j in range(4)] for s in range(2)]
         w1r = [keep.tile([P, 4, H], F32, name="w1r%d" % s) for s in range(2)]
-        w2r = [keep.tile([P, 4, N // 2], F32, name="w2r%d" % h) for h in range(2)]
+        w2r = keep.tile([P, 4, N], F32, name="w2r")
 
-        nc.sync.dma_start(w1r[0][:], w1v[0])
         nc.sync.dma_start(x[0][0][:], xv[0, 0])
         nc.sync.dma_start(x[0][1][:], xv[0, 1])
+        nc.sync.dma_start(w1r[0][:], w1v[0])
         nc.sync.dma_start(x[0][2][:], xv[0, 2])
         nc.sync.dma_start(x[0][3][:], xv[0, 3])
         nc.sync.dma_start(x[1][0][:], xv[1, 0])
@@ -49,9 +49,8 @@ def tile_picked_pick_mlp_relu2_srt_e_kernel(tc, xT, w1, w2, offs, out):
         nc.sync.dma_start(x[1][1][:], xv[1, 1])
         nc.sync.dma_start(x[1][2][:], xv[1, 2])
         nc.sync.dma_start(x[1][3][:, 0:HEAD], xv[1, 3][:, 0:HEAD])
-        nc.sync.dma_start(w2r[0][:], w2v[:, :, 0:256])
         nc.sync.dma_start(x[1][3][:, HEAD:T], xv[1, 3][:, HEAD:T])
-        nc.sync.dma_start(w2r[1][:], w2v[:, :, 256:512])
+        nc.sync.dma_start(w2r[:], w2v)
 
         g0 = keep.tile([P, 4, S], F32, name="g0")
         xb = [keep.tile([P, S, 4], BF16, name="xb%d" % s, align_bytes=64) for s in range(2)]
@@ -131,6 +130,34 @@ def tile_picked_pick_mlp_relu2_srt_e_kernel(tc, xT, w1, w2, offs, out):
                     )
             return bank
 
+        def mm1_pass(c, s, t, bank):
+            nc.tensor.matmul_mx(
+                out=bank,
+                lhsT=w1c[s][:, P * t : P * (t + 1)].bitcast(FP8X4),
+                lhsT_scale=w1s[s][:, P * t : P * (t + 1)],
+                rhs=xc[s][:, cols(c)].bitcast(FP8X4),
+                rhs_scale=xs[s][:, cols(c)],
+                start=(s == 0),
+                stop=(s == 1),
+            )
+
+        b0 = {}
+
+        def mm1_first(c):
+            for t in range(4):
+                bank = psum.tile([P, 2, CH], F32, name="bank")
+                mm1_pass(c, 0, t, bank[:, 0, :])
+                b0[c, t] = bank
+
+        def mm1_second(c, t):
+            mm1_pass(c, 1, t, b0[c, t][:, 0, :])
+
+        def relu1(c, t, on_vector):
+            if on_vector:
+                nc.vector.tensor_scalar_max(r[c][:, t, :], b0[c, t][:, 0, :], 0.0)
+            else:
+                nc.scalar.activation(r[c][:, t, :], b0[c, t][:, 0, :], RELU)
+
         def relu(c, b, bank, on_vector):
             if on_vector:
                 nc.vector.tensor_scalar_max(r[c][:, 2 * b : 2 * b + 2, :], bank[:], 0.0)
@@ -170,68 +197,79 @@ def tile_picked_pick_mlp_relu2_srt_e_kernel(tc, xT, w1, w2, offs, out):
         ov = out.rearrange("(b i p) n -> b p i n", b=2, i=2)
         b1, b2 = {}, {}
 
-        w1_copy(0, 0, nc.vector.tensor_copy)
-        w1_copy(0, 1, nc.scalar.copy)
         gather0(0)
-        w1_quant(0)
+        w1_copy(0, 0, nc.scalar.copy)
+        w1_copy(0, 1, nc.scalar.copy)
         gather0(1)
+        w1_quant(0)
         gather0(2)
         gather0(3)
         interleave(nc.scalar.copy, xb[0][:, cols(0), :], g0[:, :, cols(0)])
-        interleave(nc.vector.tensor_copy, xb[0][:, cols(1), :], g0[:, :, cols(1)])
+        interleave(nc.scalar.copy, xb[0][:, cols(1), :], g0[:, :, cols(1)])
         interleave(nc.scalar.copy, xb[0][:, cols(2), :], g0[:, :, cols(2)])
         gather1(0)
-        w1_copy(1, 0, nc.vector.tensor_copy)
-        w1_copy(1, 1, nc.scalar.copy)
         x_quant(0, 0)
         x_quant(0, 1)
+        w1_copy(1, 0, nc.scalar.copy)
+        w1_copy(1, 1, nc.scalar.copy)
         x_quant(0, 2)
-        w1_quant(1)
+        mm1_first(0)
+        mm1_first(1)
         gather1(1)
+        w1_quant(1)
         gather1(2)
         gather_part(3, 0)
         x_quant(1, 0)
-        interleave(nc.scalar.copy, w2b[0][:], w2r[0][:])
-        b1[0,0] = mm1(0, 0)
-        b1[0,1] = mm1(0, 1)
         gather_part(3, 1)
-        relu(0, 0, b1[0,0], False)
-        gather_part(3, 2)
-        relu(0, 1, b1[0,1], False)
+        mm1_second(0, 0)
+        mm1_second(0, 1)
+        mm1_second(0, 2)
+        mm1_second(0, 3)
+        relu1(0, 0, False)
+        relu1(0, 1, False)
+        relu1(0, 2, False)
+        relu1(0, 3, False)
         x_quant(1, 1)
-        b1[1,0] = mm1(1, 0)
-        b1[1,1] = mm1(1, 1)
-        interleave(nc.vector.tensor_copy, w2b[1][:], w2r[1][:])
+        gather_part(3, 2)
+        mm1_second(1, 0)
+        mm1_second(1, 1)
+        mm1_second(1, 2)
+        mm1_second(1, 3)
         x_quant(1, 2)
-        square(0, 0, False)
+        square(0, 0, True)
         square(0, 1, False)
-        relu(1, 0, b1[1,0], False)
-        relu(1, 1, b1[1,1], True)
+        relu1(1, 0, False)
+        relu1(1, 1, False)
+        relu1(1, 2, False)
+        relu1(1, 3, True)
+        interleave(nc.scalar.copy, w2b[0][:, 0:128, :], w2r[:, :, 0:128])
+        interleave(nc.scalar.copy, w2b[0][:, 128:256, :], w2r[:, :, 128:256])
+        interleave(nc.vector.tensor_copy, w2b[1][:, 0:256, :], w2r[:, :, 256:512])
+        h_quant(0)
         b1[2,0] = mm1(2, 0)
         b1[2,1] = mm1(2, 1)
         w2_quant(0)
         w2_quant(1)
-        h_quant(0)
-        square(1, 0, True)
-        square(1, 1, False)
-        relu(2, 0, b1[2,0], False)
-        relu(2, 1, b1[2,1], True)
         b2[0,0] = mm2(0, 0)
         b2[0,1] = mm2(0, 1)
+        square(1, 0, True)
+        square(1, 1, False)
         h_quant(1)
+        relu(2, 0, b1[2,0], False)
+        relu(2, 1, b1[2,1], True)
         nc.scalar.copy(y[0][0][:], b2[0,0][:])
         nc.vector.tensor_copy(y[0][1][:], b2[0,1][:])
         nc.sync.dma_start(ov[0][:, :, cols(0)], y[0][0][:])
         nc.sync.dma_start(ov[1][:, :, cols(0)], y[0][1][:])
-        square(2, 0, False)
-        square(2, 1, True)
         b2[1,0] = mm2(1, 0)
         b2[1,1] = mm2(1, 1)
+        square(2, 0, True)
+        square(2, 1, False)
+        h_quant(2)
         nc.scalar.copy(y[1][0][:], b2[1,0][:])
         nc.vector.tensor_copy(y[1][1][:], b2[1,1][:])
         nc.sync.dma_start(ov[0][:, :, cols(1)], y[1][0][:])
         nc.sync.dma_start(ov[1][:, :, cols(1)], y[1][1][:])
-        h_quant(2)
         b2[2,0] = mm2(2, 0)
         b2[2,1] = mm2(2, 1)
         nc.vector.tensor_copy(y[2][0][:], b2[2,0][:])

@@ -11,64 +11,69 @@ U32 = mybir.dt.uint32
 U16 = mybir.dt.uint16
 U8 = mybir.dt.uint8
 FP8X4 = mybir.dt.float8_e4m3fn_x4
-SQUARE = mybir.ActivationFunctionType.Square
 RELU = mybir.ActivationFunctionType.Relu
+SQUARE = mybir.ActivationFunctionType.Square
 MULT = mybir.AluOpType.mult
 
 P = 128
 CH = 256
-NCH = S // CH
-HEAD = 1536
+CHUNKS = S // CH
+HEAD = T - S + CH
 
 
 def tile_picked_pick_mlp_relu2_srt_e_kernel(tc, xT, w1, w2, offs, out):
     nc = tc.nc
     with ExitStack() as ctx:
-        lists = ctx.enter_context(tc.tile_pool(name="lists", bufs=1))
         keep = ctx.enter_context(tc.tile_pool(name="keep", bufs=1))
         psum = ctx.enter_context(tc.psum_pool(name="psum", bufs=8))
 
-        offs_t = lists.tile([P, S // 16], U16, name="offs_t")
-        nc.sync.dma_start(offs_t[:], offs)
+        x_view = xT.rearrange("(s p j) t -> s j p t", s=2, j=4)
+        w1_view = w1.rearrange("(s p j) c -> s p j c", s=2, j=4)
+        w2_view = w2.rearrange("(p j) c -> p j c", j=4)
+        out_view = out.rearrange("(b i p) n -> b p i n", b=2, i=2)
 
-        xv = xT.rearrange("(s p j) t -> s j p t", s=2, j=4)
-        w1v = w1.rearrange("(s p j) c -> s p j c", s=2, j=4)
-        w2v = w2.rearrange("(p j) c -> p j c", j=4)
-
+        offsets = keep.tile([P, S // 16], U16, name="offsets")
         x = [[keep.tile([P, T], F32, name="x%d%d" % (s, j)) for j in range(4)] for s in range(2)]
-        w1r = [keep.tile([P, 4, H], F32, name="w1r%d" % s) for s in range(2)]
-        w2r = keep.tile([P, 4, N], F32, name="w2r")
+        w1_raw = [keep.tile([P, 4, H], F32, name="w1_raw%d" % s) for s in range(2)]
+        w2_raw = keep.tile([P, 4, N], F32, name="w2_raw")
 
-        nc.sync.dma_start(x[0][0][:], xv[0, 0])
-        nc.sync.dma_start(x[0][1][:], xv[0, 1])
-        nc.sync.dma_start(w1r[0][:], w1v[0])
-        nc.sync.dma_start(x[0][2][:], xv[0, 2])
-        nc.sync.dma_start(x[0][3][:], xv[0, 3])
-        nc.sync.dma_start(x[1][0][:], xv[1, 0])
-        nc.sync.dma_start(w1r[1][:], w1v[1])
-        nc.sync.dma_start(x[1][1][:], xv[1, 1])
-        nc.sync.dma_start(x[1][2][:], xv[1, 2])
-        nc.sync.dma_start(x[1][3][:, 0:HEAD], xv[1, 3][:, 0:HEAD])
-        nc.sync.dma_start(x[1][3][:, HEAD:T], xv[1, 3][:, HEAD:T])
-        nc.sync.dma_start(w2r[:], w2v)
+        def load_x(s, j):
+            nc.sync.dma_start(x[s][j][:], x_view[s, j])
 
-        g0 = keep.tile([P, 4, S], F32, name="g0")
-        xb = [keep.tile([P, S, 4], BF16, name="xb%d" % s, align_bytes=64) for s in range(2)]
-        xc = [keep.tile([P, S], U32, name="xc%d" % s, align_bytes=64) for s in range(2)]
-        xs = [keep.tile([P, S], U8, name="xs%d" % s, align_bytes=64) for s in range(2)]
-        w1b = [keep.tile([P, H * 4], BF16, name="w1b%d" % s, align_bytes=64) for s in range(2)]
-        w1c = [keep.tile([P, H], U32, name="w1c%d" % s, align_bytes=64) for s in range(2)]
-        w1s = [keep.tile([P, H], U8, name="w1s%d" % s, align_bytes=64) for s in range(2)]
-        w2b = [keep.tile([P, N // 2, 4], BF16, name="w2b%d" % h, align_bytes=64) for h in range(2)]
-        w2c = [keep.tile([P, N // 2], U32, name="w2c%d" % h, align_bytes=64) for h in range(2)]
-        w2s = [keep.tile([P, N // 2], U8, name="w2s%d" % h, align_bytes=64) for h in range(2)]
-        r = [keep.tile([P, 4, CH], F32, name="r%d" % c) for c in range(NCH)]
-        hb = [keep.tile([P, CH, 4], BF16, name="hb%d" % c, align_bytes=64) for c in range(NCH)]
-        hc = [keep.tile([P, CH], U32, name="hc%d" % c, align_bytes=64) for c in range(NCH)]
-        hs = [keep.tile([P, CH], U8, name="hs%d" % c, align_bytes=64) for c in range(NCH)]
-        y = [[keep.tile([P, 2, CH], F32, name="y%d%d" % (c, b)) for b in range(2)] for c in range(NCH)]
+        def load_w1(s):
+            nc.sync.dma_start(w1_raw[s][:], w1_view[s])
 
-        def cols(c):
+        load_x(0, 0)
+        nc.sync.dma_start(offsets[:], offs)
+        load_x(0, 1)
+        load_w1(0)
+        load_x(0, 2)
+        load_x(0, 3)
+        load_x(1, 0)
+        load_w1(1)
+        load_x(1, 1)
+        load_x(1, 2)
+        for cols in (slice(0, HEAD), slice(HEAD, T)):
+            nc.sync.dma_start(x[1][3][:, cols], x_view[1, 3][:, cols])
+        nc.sync.dma_start(w2_raw[:], w2_view)
+
+        picked = [keep.tile([P, 4, S], F32, name="picked%d" % s) for s in range(2)]
+        x_bf = [keep.tile([P, S, 4], BF16, name="x_bf%d" % s, align_bytes=64) for s in range(2)]
+        x_codes = [keep.tile([P, S], U32, name="x_codes%d" % s, align_bytes=64) for s in range(2)]
+        x_scales = [keep.tile([P, S], U8, name="x_scales%d" % s, align_bytes=64) for s in range(2)]
+        w1_bf = [keep.tile([P, 4 * H], BF16, name="w1_bf%d" % s, align_bytes=64) for s in range(2)]
+        w1_codes = [keep.tile([P, H], U32, name="w1_codes%d" % s, align_bytes=64) for s in range(2)]
+        w1_scales = [keep.tile([P, H], U8, name="w1_scales%d" % s, align_bytes=64) for s in range(2)]
+        w2_bf = keep.tile([P, N, 4], BF16, name="w2_bf", align_bytes=64)
+        w2_codes = keep.tile([P, N], U32, name="w2_codes", align_bytes=64)
+        w2_scales = keep.tile([P, N], U8, name="w2_scales", align_bytes=64)
+        r = [keep.tile([P, 4, n], F32, name="r%d" % n) for n in (CH, S - CH)]
+        h_bf = [keep.tile([P, CH, 4], BF16, name="h_bf%d" % c, align_bytes=64) for c in range(CHUNKS)]
+        h_codes = [keep.tile([P, CH], U32, name="h_codes%d" % c, align_bytes=64) for c in range(CHUNKS)]
+        h_scales = [keep.tile([P, CH], U8, name="h_scales%d" % c, align_bytes=64) for c in range(CHUNKS)]
+        y = [[keep.tile([P, 2, CH], F32, name="y%d%d" % (c, b)) for b in range(2)] for c in range(CHUNKS)]
+
+        def chunk(c):
             return slice(CH * c, CH * (c + 1))
 
         def interleave(copy, dst, src):
@@ -77,202 +82,182 @@ def tile_picked_pick_mlp_relu2_srt_e_kernel(tc, xT, w1, w2, offs, out):
                 in_=src.rearrange("p t (c i) -> p c t i", i=4),
             )
 
-        def w1_copy(s, h, copy):
-            ms = slice(64 * h, 64 * (h + 1))
-            copy(
-                out=w1b[s][:].rearrange("p (t m j) -> p m j t", t=4, j=4)[:, ms],
-                in_=w1r[s][:].rearrange("p j (m t) -> p m j t", t=4)[:, ms],
-            )
+        def quantize(codes, scales, values):
+            nc.vector.quantize_mx(out=codes.bitcast(FP8X4), scales=scales, in_=values)
 
-        def w1_quant(s):
-            nc.vector.quantize_mx(out=w1c[s][:].bitcast(FP8X4), scales=w1s[s][:], in_=w1b[s][:])
+        def gather(s, j):
+            nc.vector.tensor_copy(picked[s][:, j, :], x[s][j][:].indirect(offsets[:]))
 
-        def x_quant(s, c):
-            nc.vector.quantize_mx(
-                out=xc[s][:, cols(c)].bitcast(FP8X4),
-                scales=xs[s][:, cols(c)],
-                in_=xb[s][:, cols(c), :].rearrange("p n t -> p (n t)"),
-            )
-
-        def gather0(j):
-            nc.vector.tensor_copy(g0[:, j, :], x[0][j][:].indirect(offs_t[:]))
-
-        def gather1(j):
-            nc.vector.tensor_copy(xb[1][:, :, j], x[1][j][:].indirect(offs_t[:]))
-
-        def gather_part(j, c):
-            width = HEAD if c == 0 else T
+        def gather_part(first, last, width):
             nc.vector.tensor_copy(
-                xb[1][:, cols(c), j],
-                x[1][j][:, 0:width].indirect(offs_t[:, CH // 16 * c : CH // 16 * (c + 1)]),
+                picked[1][:, 3, first:last],
+                x[1][3][:, 0:width].indirect(offsets[:, first // 16 : last // 16]),
             )
 
-        def w2_quant(h):
-            nc.vector.quantize_mx(
-                out=w2c[h][:].bitcast(FP8X4),
-                scales=w2s[h][:],
-                in_=w2b[h][:].rearrange("p n t -> p (n t)"),
+        def x_interleave(copy, s, c):
+            interleave(copy, x_bf[s][:, chunk(c), :], picked[s][:, :, chunk(c)])
+
+        def x_quantize(s, c):
+            quantize(
+                x_codes[s][:, chunk(c)],
+                x_scales[s][:, chunk(c)],
+                x_bf[s][:, chunk(c), :].rearrange("p n t -> p (n t)"),
             )
 
-        def mm1(c, b):
-            bank = psum.tile([P, 2, CH], F32, name="bank")
-            for i in range(2):
-                t = 2 * b + i
-                for s in range(2):
-                    nc.tensor.matmul_mx(
-                        out=bank[:, i, :],
-                        lhsT=w1c[s][:, P * t : P * (t + 1)].bitcast(FP8X4),
-                        lhsT_scale=w1s[s][:, P * t : P * (t + 1)],
-                        rhs=xc[s][:, cols(c)].bitcast(FP8X4),
-                        rhs_scale=xs[s][:, cols(c)],
-                        start=(s == 0),
-                        stop=(s == 1),
-                    )
-            return bank
+        def w1_interleave(copy, s, half):
+            tiles = slice(2 * half, 2 * half + 2)
+            copy(
+                out=w1_bf[s][:].rearrange("p (t m j) -> p m t j", t=4, j=4)[:, :, tiles, :],
+                in_=w1_raw[s][:].rearrange("p j (m t) -> p m t j", t=4)[:, :, tiles, :],
+            )
 
-        def mm1_pass(c, s, t, bank):
+        def w1_quantize(s):
+            quantize(w1_codes[s][:], w1_scales[s][:], w1_bf[s][:])
+
+        def w2_interleave(copy, q):
+            n = slice(P * q, P * (q + 1))
+            interleave(copy, w2_bf[:, n, :], w2_raw[:, :, n])
+
+        def w2_quantize(half):
+            n = slice(N // 2 * half, N // 2 * (half + 1))
+            quantize(w2_codes[:, n], w2_scales[:, n], w2_bf[:, n, :].rearrange("p n t -> p (n t)"))
+
+        group_cols = [slice(0, CH), slice(CH, S)]
+        banks = [[], []]
+
+        def mm1(g, s, t):
+            cols = group_cols[g]
+            width = cols.stop - cols.start
+            if s == 0:
+                bank = psum.tile([P, 512], F32, name="bank")
+                banks[g].append(bank)
+            block = slice(P * t, P * (t + 1))
             nc.tensor.matmul_mx(
-                out=bank,
-                lhsT=w1c[s][:, P * t : P * (t + 1)].bitcast(FP8X4),
-                lhsT_scale=w1s[s][:, P * t : P * (t + 1)],
-                rhs=xc[s][:, cols(c)].bitcast(FP8X4),
-                rhs_scale=xs[s][:, cols(c)],
+                out=banks[g][t][:, 0:width],
+                lhsT=w1_codes[s][:, block].bitcast(FP8X4),
+                lhsT_scale=w1_scales[s][:, block],
+                rhs=x_codes[s][:, cols].bitcast(FP8X4),
+                rhs_scale=x_scales[s][:, cols],
                 start=(s == 0),
                 stop=(s == 1),
             )
 
-        b0 = {}
+        def relu_scalar(g, t):
+            width = r[g].shape[2]
+            nc.scalar.activation(r[g][:, t, :], banks[g][t][:, 0:width], RELU)
 
-        def mm1_first(c):
-            for t in range(4):
-                bank = psum.tile([P, 2, CH], F32, name="bank")
-                mm1_pass(c, 0, t, bank[:, 0, :])
-                b0[c, t] = bank
+        def relu_vector(g, t):
+            width = r[g].shape[2]
+            nc.vector.tensor_scalar_max(r[g][:, t, :], banks[g][t][:, 0:width], 0.0)
 
-        def mm1_second(c, t):
-            mm1_pass(c, 1, t, b0[c, t][:, 0, :])
+        def square_views(c, half):
+            g = 0 if c == 0 else 1
+            first = CH * c - group_cols[g].start + CH // 2 * half
+            src = r[g][:, :, first : first + CH // 2].rearrange("p t (c i) -> p c t i", i=4)
+            n = slice(CH // 2 * half, CH // 2 * (half + 1))
+            return h_bf[c][:, n, :].rearrange("p (c i) t -> p c t i", i=4), src
 
-        def relu1(c, t, on_vector):
-            if on_vector:
-                nc.vector.tensor_scalar_max(r[c][:, t, :], b0[c, t][:, 0, :], 0.0)
-            else:
-                nc.scalar.activation(r[c][:, t, :], b0[c, t][:, 0, :], RELU)
+        def square_scalar(c, half):
+            dst, src = square_views(c, half)
+            nc.scalar.activation(dst, src, SQUARE)
 
-        def relu(c, b, bank, on_vector):
-            if on_vector:
-                nc.vector.tensor_scalar_max(r[c][:, 2 * b : 2 * b + 2, :], bank[:], 0.0)
-            else:
-                nc.scalar.activation(r[c][:, 2 * b : 2 * b + 2, :], bank[:], RELU)
+        def square_vector(c, half):
+            dst, src = square_views(c, half)
+            nc.vector.tensor_tensor(dst, src, src, MULT)
 
-        def square(c, h, on_vector):
-            n = slice(CH // 2 * h, CH // 2 * (h + 1))
-            rv = r[c][:, :, n].rearrange("p t (c i) -> p c t i", i=4)
-            hv = hb[c][:, n, :].rearrange("p (c i) t -> p c t i", i=4)
-            if on_vector:
-                nc.vector.tensor_tensor(hv, rv, rv, MULT)
-            else:
-                nc.scalar.activation(hv, rv, SQUARE)
+        def h_quantize(c):
+            quantize(h_codes[c][:], h_scales[c][:], h_bf[c][:].rearrange("p n t -> p (n t)"))
 
-        def h_quant(c):
-            nc.vector.quantize_mx(
-                out=hc[c][:].bitcast(FP8X4),
-                scales=hs[c][:],
-                in_=hb[c][:].rearrange("p n t -> p (n t)"),
-            )
+        y_banks = {}
 
         def mm2(c, b):
-            bank = psum.tile([P, 2, CH], F32, name="bank")
+            bank = psum.tile([P, 512], F32, name="bank")
             for i in range(2):
+                block = slice(P * (2 * b + i), P * (2 * b + i + 1))
                 nc.tensor.matmul_mx(
-                    out=bank[:, i, :],
-                    lhsT=w2c[b][:, P * i : P * (i + 1)].bitcast(FP8X4),
-                    lhsT_scale=w2s[b][:, P * i : P * (i + 1)],
-                    rhs=hc[c][:].bitcast(FP8X4),
-                    rhs_scale=hs[c][:],
+                    out=bank[:, CH * i : CH * (i + 1)],
+                    lhsT=w2_codes[:, block].bitcast(FP8X4),
+                    lhsT_scale=w2_scales[:, block],
+                    rhs=h_codes[c][:].bitcast(FP8X4),
+                    rhs_scale=h_scales[c][:],
                     start=True,
                     stop=True,
                 )
-            return bank
+            y_banks[c, b] = bank
 
-        ov = out.rearrange("(b i p) n -> b p i n", b=2, i=2)
-        b1, b2 = {}, {}
+        def store(copy, c, b):
+            copy(out=y[c][b][:].rearrange("p i n -> p (i n)"), in_=y_banks[c, b][:])
+            nc.sync.dma_start(out_view[b][:, :, chunk(c)], y[c][b][:])
 
-        gather0(0)
-        w1_copy(0, 0, nc.scalar.copy)
-        w1_copy(0, 1, nc.scalar.copy)
-        gather0(1)
-        w1_quant(0)
-        gather0(2)
-        gather0(3)
-        interleave(nc.scalar.copy, xb[0][:, cols(0), :], g0[:, :, cols(0)])
-        interleave(nc.scalar.copy, xb[0][:, cols(1), :], g0[:, :, cols(1)])
-        interleave(nc.scalar.copy, xb[0][:, cols(2), :], g0[:, :, cols(2)])
-        gather1(0)
-        x_quant(0, 0)
-        x_quant(0, 1)
-        w1_copy(1, 0, nc.scalar.copy)
-        w1_copy(1, 1, nc.scalar.copy)
-        x_quant(0, 2)
-        mm1_first(0)
-        mm1_first(1)
-        gather1(1)
-        w1_quant(1)
-        gather1(2)
-        gather_part(3, 0)
-        x_quant(1, 0)
-        gather_part(3, 1)
-        mm1_second(0, 0)
-        mm1_second(0, 1)
-        mm1_second(0, 2)
-        mm1_second(0, 3)
-        relu1(0, 0, False)
-        relu1(0, 1, False)
-        relu1(0, 2, False)
-        relu1(0, 3, False)
-        x_quant(1, 1)
-        gather_part(3, 2)
-        mm1_second(1, 0)
-        mm1_second(1, 1)
-        mm1_second(1, 2)
-        mm1_second(1, 3)
-        x_quant(1, 2)
-        square(0, 0, True)
-        square(0, 1, False)
-        relu1(1, 0, False)
-        relu1(1, 1, False)
-        relu1(1, 2, False)
-        relu1(1, 3, True)
-        interleave(nc.scalar.copy, w2b[0][:, 0:128, :], w2r[:, :, 0:128])
-        interleave(nc.scalar.copy, w2b[0][:, 128:256, :], w2r[:, :, 128:256])
-        interleave(nc.vector.tensor_copy, w2b[1][:, 0:256, :], w2r[:, :, 256:512])
-        h_quant(0)
-        b1[2,0] = mm1(2, 0)
-        b1[2,1] = mm1(2, 1)
-        w2_quant(0)
-        w2_quant(1)
-        b2[0,0] = mm2(0, 0)
-        b2[0,1] = mm2(0, 1)
-        square(1, 0, True)
-        square(1, 1, False)
-        h_quant(1)
-        relu(2, 0, b1[2,0], False)
-        relu(2, 1, b1[2,1], True)
-        nc.scalar.copy(y[0][0][:], b2[0,0][:])
-        nc.vector.tensor_copy(y[0][1][:], b2[0,1][:])
-        nc.sync.dma_start(ov[0][:, :, cols(0)], y[0][0][:])
-        nc.sync.dma_start(ov[1][:, :, cols(0)], y[0][1][:])
-        b2[1,0] = mm2(1, 0)
-        b2[1,1] = mm2(1, 1)
-        square(2, 0, True)
-        square(2, 1, False)
-        h_quant(2)
-        nc.scalar.copy(y[1][0][:], b2[1,0][:])
-        nc.vector.tensor_copy(y[1][1][:], b2[1,1][:])
-        nc.sync.dma_start(ov[0][:, :, cols(1)], y[1][0][:])
-        nc.sync.dma_start(ov[1][:, :, cols(1)], y[1][1][:])
-        b2[2,0] = mm2(2, 0)
-        b2[2,1] = mm2(2, 1)
-        nc.vector.tensor_copy(y[2][0][:], b2[2,0][:])
-        nc.scalar.copy(y[2][1][:], b2[2,1][:])
-        nc.sync.dma_start(ov[0][:, :, cols(2)], y[2][0][:])
-        nc.sync.dma_start(ov[1][:, :, cols(2)], y[2][1][:])
+        on_scalar = nc.scalar.copy
+        on_vector = nc.vector.tensor_copy
+
+        gather(0, 0)
+        w1_interleave(on_scalar, 0, 0)
+        w1_interleave(on_scalar, 0, 1)
+        gather(0, 1)
+        w1_quantize(0)
+        gather(0, 2)
+        gather(0, 3)
+        for c in range(CHUNKS):
+            x_interleave(on_scalar, 0, c)
+        gather(1, 0)
+        x_quantize(0, 0)
+        x_quantize(0, 1)
+        w1_interleave(on_scalar, 1, 0)
+        w1_interleave(on_scalar, 1, 1)
+        gather(1, 1)
+        for t in range(4):
+            mm1(0, 0, t)
+        x_quantize(0, 2)
+        for t in range(4):
+            mm1(1, 0, t)
+        w1_quantize(1)
+        gather(1, 2)
+
+        gather_part(0, CH, HEAD)
+        gather_part(CH, S, T)
+        x_interleave(on_scalar, 1, 0)
+        x_interleave(on_vector, 1, 1)
+        x_interleave(on_scalar, 1, 2)
+        for c in range(CHUNKS):
+            x_quantize(1, c)
+        w2_interleave(on_vector, 2)
+        w2_interleave(on_vector, 1)
+        w2_interleave(on_scalar, 0)
+        for t in range(4):
+            mm1(0, 1, t)
+        relu_scalar(0, 0)
+        relu_vector(0, 1)
+        relu_scalar(0, 2)
+        relu_scalar(0, 3)
+        w2_quantize(0)
+        for t in range(4):
+            mm1(1, 1, t)
+        relu_scalar(1, 0)
+        square_scalar(0, 0)
+        square_vector(0, 1)
+        relu_vector(1, 1)
+        relu_scalar(1, 2)
+        relu_vector(1, 3)
+        h_quantize(0)
+        w2_interleave(on_scalar, 3)
+        w2_quantize(1)
+        square_vector(1, 0)
+        square_scalar(1, 1)
+        h_quantize(1)
+        square_vector(2, 0)
+        square_scalar(2, 1)
+        mm2(0, 0)
+        mm2(0, 1)
+        store(on_scalar, 0, 0)
+        store(on_scalar, 0, 1)
+        mm2(1, 0)
+        mm2(1, 1)
+        h_quantize(2)
+        store(on_vector, 1, 0)
+        store(on_scalar, 1, 1)
+        mm2(2, 0)
+        mm2(2, 1)
+        store(on_scalar, 2, 0)
+        store(on_vector, 2, 1)

@@ -25,6 +25,7 @@ def tile_picked_pick_mlp_relu2_srt_e_kernel(tc, xT, w1, w2, offs, out):
     nc = tc.nc
     with ExitStack() as ctx:
         keep = ctx.enter_context(tc.tile_pool(name="keep", bufs=1))
+        turns = ctx.enter_context(tc.tile_pool(name="turns", bufs=1))
         psum = ctx.enter_context(tc.psum_pool(name="psum", bufs=8))
 
         x_view = xT.rearrange("(s p j) t -> s j p t", s=2, j=4)
@@ -58,13 +59,15 @@ def tile_picked_pick_mlp_relu2_srt_e_kernel(tc, xT, w1, w2, offs, out):
         nc.sync.dma_start(w2_raw[:], w2_view)
 
         picked = [keep.tile([P, 4, S], F32, name="picked%d" % s) for s in range(2)]
-        x_bf = [keep.tile([P, S, 4], BF16, name="x_bf%d" % s, align_bytes=64) for s in range(2)]
+        x_bf = [
+            keep.tile([P, S, 4], BF16, name="x_bf0", align_bytes=64),
+            turns.tile([P, S, 4], BF16, name="x_bf1", tag="bf", align_bytes=64),
+        ]
         x_codes = [keep.tile([P, S], U32, name="x_codes%d" % s, align_bytes=64) for s in range(2)]
         x_scales = [keep.tile([P, S], U8, name="x_scales%d" % s, align_bytes=64) for s in range(2)]
         w1_bf = [keep.tile([P, 4 * H], BF16, name="w1_bf%d" % s, align_bytes=64) for s in range(2)]
         w1_codes = [keep.tile([P, H], U32, name="w1_codes%d" % s, align_bytes=64) for s in range(2)]
         w1_scales = [keep.tile([P, H], U8, name="w1_scales%d" % s, align_bytes=64) for s in range(2)]
-        w2_bf = keep.tile([P, N, 4], BF16, name="w2_bf", align_bytes=64)
         w2_codes = keep.tile([P, N], U32, name="w2_codes", align_bytes=64)
         w2_scales = keep.tile([P, N], U8, name="w2_scales", align_bytes=64)
         r = [keep.tile([P, 4, n], F32, name="r%d" % n) for n in (CH, S - CH)]
@@ -114,11 +117,15 @@ def tile_picked_pick_mlp_relu2_srt_e_kernel(tc, xT, w1, w2, offs, out):
         def w1_quantize(s):
             quantize(w1_codes[s][:], w1_scales[s][:], w1_bf[s][:])
 
+        w2_bf_tile = []
+
         def w2_interleave(copy, q):
+            w2_bf = w2_bf_tile[0]
             n = slice(P * q, P * (q + 1))
             interleave(copy, w2_bf[:, n, :], w2_raw[:, :, n])
 
         def w2_quantize(half):
+            w2_bf = w2_bf_tile[0]
             n = slice(N // 2 * half, N // 2 * (half + 1))
             quantize(w2_codes[:, n], w2_scales[:, n], w2_bf[:, n, :].rearrange("p n t -> p (n t)"))
 
@@ -199,8 +206,9 @@ def tile_picked_pick_mlp_relu2_srt_e_kernel(tc, xT, w1, w2, offs, out):
         w1_quantize(0)
         gather(0, 2)
         gather(0, 3)
-        for c in range(CHUNKS):
-            x_interleave(on_scalar, 0, c)
+        x_interleave(on_scalar, 0, 0)
+        x_interleave(on_vector, 0, 1)
+        x_interleave(on_scalar, 0, 2)
         gather(1, 0)
         x_quantize(0, 0)
         x_quantize(0, 1)
@@ -218,22 +226,24 @@ def tile_picked_pick_mlp_relu2_srt_e_kernel(tc, xT, w1, w2, offs, out):
         gather_part(0, CH, HEAD)
         gather_part(CH, S, T)
         x_interleave(on_scalar, 1, 0)
-        x_interleave(on_vector, 1, 1)
-        x_interleave(on_scalar, 1, 2)
+        x_interleave(on_scalar, 1, 1)
+        x_interleave(on_vector, 1, 2)
         for c in range(CHUNKS):
             x_quantize(1, c)
-        w2_interleave(on_vector, 2)
-        w2_interleave(on_vector, 1)
-        w2_interleave(on_scalar, 0)
         for t in range(4):
             mm1(0, 1, t)
         relu_scalar(0, 0)
         relu_vector(0, 1)
         relu_scalar(0, 2)
         relu_scalar(0, 3)
-        w2_quantize(0)
         for t in range(4):
             mm1(1, 1, t)
+        w2_bf = turns.tile([P, N, 4], BF16, name="w2_bf", tag="bf", align_bytes=64)
+        w2_bf_tile.append(w2_bf)
+        w2_interleave(on_vector, 2)
+        w2_interleave(on_vector, 1)
+        w2_interleave(on_scalar, 0)
+        w2_quantize(0)
         relu_scalar(1, 0)
         square_scalar(0, 0)
         square_vector(0, 1)

from contextlib import ExitStack

import concourse.mybir as mybir

K, T, S, H, N = 1024, 2048, 768, 512, 512
FLOPS = 2 * S * (K * H + H * N)

F32 = mybir.dt.float32
BF16 = mybir.dt.bfloat16
U32 = mybir.dt.uint32
U16 = mybir.dt.uint16
U8 = mybir.dt.uint8
FP8X4 = mybir.dt.float8_e4m3fn_x4
RELU = mybir.ActivationFunctionType.Relu
SQUARE = mybir.ActivationFunctionType.Square
MULT = mybir.AluOpType.mult

P = 128
CH = 256
CHUNKS = S // CH
HEAD = T - S + CH


def tile_picked_pick_mlp_relu2_srt_e_kernel(tc, xT, w1, w2, offs, out):
    nc = tc.nc
    with ExitStack() as ctx:
        keep = ctx.enter_context(tc.tile_pool(name="keep", bufs=1))
        turns = ctx.enter_context(tc.tile_pool(name="turns", bufs=1))
        psum = ctx.enter_context(tc.psum_pool(name="psum", bufs=8))

        x_view = xT.rearrange("(s p j) t -> s j p t", s=2, j=4)
        w1_view = w1.rearrange("(s p j) c -> s p j c", s=2, j=4)
        w2_view = w2.rearrange("(p j) c -> p j c", j=4)
        out_view = out.rearrange("(b i p) n -> b p i n", b=2, i=2)

        offsets = keep.tile([P, S // 16], U16, name="offsets")
        x = [[keep.tile([P, T], F32, name="x%d%d" % (s, j)) for j in range(4)] for s in range(2)]
        w1_raw = [keep.tile([P, 4, H], F32, name="w1_raw%d" % s) for s in range(2)]
        w2_raw = keep.tile([P, 4, N], F32, name="w2_raw")

        def load_x(s, j):
            nc.sync.dma_start(x[s][j][:], x_view[s, j])

        def load_w1(s):
            nc.sync.dma_start(w1_raw[s][:], w1_view[s])

        load_x(0, 0)
        nc.sync.dma_start(offsets[:], offs)
        load_x(0, 1)
        load_w1(0)
        load_x(0, 2)
        load_x(0, 3)
        load_x(1, 0)
        load_w1(1)
        load_x(1, 1)
        load_x(1, 2)
        for cols in (slice(0, HEAD), slice(HEAD, T)):
            nc.sync.dma_start(x[1][3][:, cols], x_view[1, 3][:, cols])
        nc.sync.dma_start(w2_raw[:], w2_view)

        picked = [keep.tile([P, 4, S], F32, name="picked%d" % s) for s in range(2)]
        x_bf = [
            keep.tile([P, S, 4], BF16, name="x_bf0", align_bytes=64),
            turns.tile([P, S, 4], BF16, name="x_bf1", tag="bf", align_bytes=64),
        ]
        x_codes = [keep.tile([P, S], U32, name="x_codes%d" % s, align_bytes=64) for s in range(2)]
        x_scales = [keep.tile([P, S], U8, name="x_scales%d" % s, align_bytes=64) for s in range(2)]
        w1_bf = [keep.tile([P, 4 * H], BF16, name="w1_bf%d" % s, align_bytes=64) for s in range(2)]
        w1_codes = [keep.tile([P, H], U32, name="w1_codes%d" % s, align_bytes=64) for s in range(2)]
        w1_scales = [keep.tile([P, H], U8, name="w1_scales%d" % s, align_bytes=64) for s in range(2)]
        w2_codes = keep.tile([P, N], U32, name="w2_codes", align_bytes=64)
        w2_scales = keep.tile([P, N], U8, name="w2_scales", align_bytes=64)
        r = [keep.tile([P, 4, n], F32, name="r%d" % n) for n in (CH, S - CH)]
        h_bf = [keep.tile([P, CH, 4], BF16, name="h_bf%d" % c, align_bytes=64) for c in range(CHUNKS)]
        h_codes = [keep.tile([P, CH], U32, name="h_codes%d" % c, align_bytes=64) for c in range(CHUNKS)]
        h_scales = [keep.tile([P, CH], U8, name="h_scales%d" % c, align_bytes=64) for c in range(CHUNKS)]
        y = [[keep.tile([P, 2, CH], F32, name="y%d%d" % (c, b)) for b in range(2)] for c in range(CHUNKS)]

        def chunk(c):
            return slice(CH * c, CH * (c + 1))

        def interleave(copy, dst, src):
            copy(
                out=dst.rearrange("p (c i) t -> p c t i", i=4),
                in_=src.rearrange("p t (c i) -> p c t i", i=4),
            )

        def quantize(codes, scales, values):
            nc.vector.quantize_mx(out=codes.bitcast(FP8X4), scales=scales, in_=values)

        def gather(s, j):
            nc.vector.tensor_copy(picked[s][:, j, :], x[s][j][:].indirect(offsets[:]))

        def gather_part(first, last, width):
            nc.vector.tensor_copy(
                picked[1][:, 3, first:last],
                x[1][3][:, 0:width].indirect(offsets[:, first // 16 : last // 16]),
            )

        def x_interleave(copy, s, c):
            interleave(copy, x_bf[s][:, chunk(c), :], picked[s][:, :, chunk(c)])

        def x_quantize(s, c):
            quantize(
                x_codes[s][:, chunk(c)],
                x_scales[s][:, chunk(c)],
                x_bf[s][:, chunk(c), :].rearrange("p n t -> p (n t)"),
            )

        def w1_interleave(copy, s, half):
            tiles = slice(2 * half, 2 * half + 2)
            copy(
                out=w1_bf[s][:].rearrange("p (t m j) -> p m t j", t=4, j=4)[:, :, tiles, :],
                in_=w1_raw[s][:].rearrange("p j (m t) -> p m t j", t=4)[:, :, tiles, :],
            )

        def w1_quantize(s):
            quantize(w1_codes[s][:], w1_scales[s][:], w1_bf[s][:])

        w2_bf_tile = []

        def w2_interleave(copy, q):
            w2_bf = w2_bf_tile[0]
            n = slice(P * q, P * (q + 1))
            interleave(copy, w2_bf[:, n, :], w2_raw[:, :, n])

        def w2_quantize(half):
            w2_bf = w2_bf_tile[0]
            n = slice(N // 2 * half, N // 2 * (half + 1))
            quantize(w2_codes[:, n], w2_scales[:, n], w2_bf[:, n, :].rearrange("p n t -> p (n t)"))

        group_cols = [slice(0, CH), slice(CH, S)]
        banks = [[], []]

        def mm1(g, s, t):
            cols = group_cols[g]
            width = cols.stop - cols.start
            if s == 0:
                bank = psum.tile([P, 512], F32, name="bank")
                banks[g].append(bank)
            block = slice(P * t, P * (t + 1))
            nc.tensor.matmul_mx(
                out=banks[g][t][:, 0:width],
                lhsT=w1_codes[s][:, block].bitcast(FP8X4),
                lhsT_scale=w1_scales[s][:, block],
                rhs=x_codes[s][:, cols].bitcast(FP8X4),
                rhs_scale=x_scales[s][:, cols],
                start=(s == 0),
                stop=(s == 1),
            )

        def relu_scalar(g, t):
            width = r[g].shape[2]
            nc.scalar.activation(r[g][:, t, :], banks[g][t][:, 0:width], RELU)

        def relu_vector(g, t):
            width = r[g].shape[2]
            nc.vector.tensor_scalar_max(r[g][:, t, :], banks[g][t][:, 0:width], 0.0)

        def square_views(c, half):
            g = 0 if c == 0 else 1
            first = CH * c - group_cols[g].start + CH // 2 * half
            src = r[g][:, :, first : first + CH // 2].rearrange("p t (c i) -> p c t i", i=4)
            n = slice(CH // 2 * half, CH // 2 * (half + 1))
            return h_bf[c][:, n, :].rearrange("p (c i) t -> p c t i", i=4), src

        def square_scalar(c, half):
            dst, src = square_views(c, half)
            nc.scalar.activation(dst, src, SQUARE)

        def square_vector(c, half):
            dst, src = square_views(c, half)
            nc.vector.tensor_tensor(dst, src, src, MULT)

        def h_quantize(c):
            quantize(h_codes[c][:], h_scales[c][:], h_bf[c][:].rearrange("p n t -> p (n t)"))

        y_banks = {}

        def mm2(c, b):
            bank = psum.tile([P, 512], F32, name="bank")
            for i in range(2):
                block = slice(P * (2 * b + i), P * (2 * b + i + 1))
                nc.tensor.matmul_mx(
                    out=bank[:, CH * i : CH * (i + 1)],
                    lhsT=w2_codes[:, block].bitcast(FP8X4),
                    lhsT_scale=w2_scales[:, block],
                    rhs=h_codes[c][:].bitcast(FP8X4),
                    rhs_scale=h_scales[c][:],
                    start=True,
                    stop=True,
                )
            y_banks[c, b] = bank

        def store(copy, c, b):
            copy(out=y[c][b][:].rearrange("p i n -> p (i n)"), in_=y_banks[c, b][:])
            nc.sync.dma_start(out_view[b][:, :, chunk(c)], y[c][b][:])

        on_scalar = nc.scalar.copy
        on_vector = nc.vector.tensor_copy

        gather(0, 0)
        w1_interleave(on_scalar, 0, 0)
        w1_interleave(on_scalar, 0, 1)
        gather(0, 1)
        w1_quantize(0)
        gather(0, 2)
        gather(0, 3)
        x_interleave(on_scalar, 0, 0)
        x_interleave(on_vector, 0, 1)
        x_interleave(on_scalar, 0, 2)
        gather(1, 0)
        x_quantize(0, 0)
        x_quantize(0, 1)
        w1_interleave(on_scalar, 1, 0)
        w1_interleave(on_scalar, 1, 1)
        gather(1, 1)
        for t in range(4):
            mm1(0, 0, t)
        x_quantize(0, 2)
        for t in range(4):
            mm1(1, 0, t)
        w1_quantize(1)
        gather(1, 2)

        gather_part(0, CH, HEAD)
        gather_part(CH, S, T)
        x_interleave(on_scalar, 1, 0)
        x_interleave(on_scalar, 1, 1)
        x_interleave(on_vector, 1, 2)
        for c in range(CHUNKS):
            x_quantize(1, c)
        for t in range(4):
            mm1(0, 1, t)
        relu_scalar(0, 0)
        relu_vector(0, 1)
        relu_scalar(0, 2)
        relu_scalar(0, 3)
        for t in range(4):
            mm1(1, 1, t)
        w2_bf = turns.tile([P, N, 4], BF16, name="w2_bf", tag="bf", align_bytes=64)
        w2_bf_tile.append(w2_bf)
        w2_interleave(on_vector, 2)
        w2_interleave(on_vector, 1)
        w2_interleave(on_scalar, 0)
        w2_quantize(0)
        relu_scalar(1, 0)
        square_scalar(0, 0)
        square_vector(0, 1)
        relu_vector(1, 1)
        relu_scalar(1, 2)
        relu_vector(1, 3)
        h_quantize(0)
        w2_interleave(on_scalar, 3)
        w2_quantize(1)
        square_vector(1, 0)
        square_scalar(1, 1)
        h_quantize(1)
        square_vector(2, 0)
        square_scalar(2, 1)
        mm2(0, 0)
        mm2(0, 1)
        store(on_scalar, 0, 0)
        store(on_scalar, 0, 1)
        mm2(1, 0)
        mm2(1, 1)
        h_quantize(2)
        store(on_vector, 1, 0)
        store(on_scalar, 1, 1)
        mm2(2, 0)
        mm2(2, 1)
        store(on_scalar, 2, 0)
        store(on_vector, 2, 1)
